import numpy as np
import ml_dtypes


def mxq(x, axis, fmt="e4m3"):
    dtype, down = {"e4m3": (ml_dtypes.float8_e4m3fn, 7), "e5m2": (ml_dtypes.float8_e5m2, 14)}[fmt]
    v = np.moveaxis(np.asarray(x, np.float32).astype(ml_dtypes.bfloat16).astype(np.float64), axis, -1)
    blocks = v.reshape(v.shape[:-1] + (-1, 32))
    amax = np.abs(blocks).max(-1, keepdims=True)
    byte = np.maximum(np.where(amax > 0, np.frexp(amax)[1] - 1 + 127, 0) - down, 1)
    scale = np.exp2(byte - 127.0)
    codes = (blocks / scale).astype(np.float32).astype(dtype).astype(np.float64)
    return np.moveaxis((codes * scale).reshape(v.shape), -1, axis)


WIDE = False


def mx_kscale(k):
    if not WIDE:
        return np.ones(k)
    levels = np.array([10, -10, 5, -5, 0])
    if k % 512:
        return np.exp2(np.random.permutation(np.resize(levels, k // 32))).repeat(32)
    a = np.empty((k // 512, 16))
    for p in range(k // 512):
        a[p, :8] = np.random.permutation(np.resize(levels, 8))
        for g in range(8):
            far = levels[np.abs(levels - a[p, g]) >= 10]
            a[p, g + 8] = far[np.random.randint(len(far))]
    return np.exp2(a.ravel()).repeat(32)


def f64(x):
    return np.asarray(x).astype(np.float64)


def striped(idx):
    return np.tile(np.asarray(idx).reshape(-1, 16).T, (8, 1)).astype(np.uint16)


def unstriped(offs):
    return offs[:16].T.reshape(-1).astype(np.int64)


E2M1 = np.array([0.0, 0.5, 1.0, 1.5, 2.0, 3.0, 4.0, 6.0, -0.0, -0.5, -1.0, -1.5, -2.0, -3.0, -4.0, -6.0])


def pack_weight(w, fmt):
    k, n = w.shape
    w = f64(np.asarray(w, np.float32).astype(ml_dtypes.bfloat16)).reshape(k // 32, 32, n)
    amax = np.abs(w).max(1)
    if fmt == "e4m3":
        byte = np.frexp(amax)[1] - 1 + 127 - 7
    else:
        mant, ex = np.frexp(amax / 6.0)
        byte = np.where(mant > 0.5, ex, ex - 1) + 127
    byte = np.clip(np.where(amax > 0, byte, 1), 1, 254)
    scaled = (w * np.exp2(127.0 - byte)[:, None, :]).reshape(k, n).astype(np.float32)
    by_word = np.ascontiguousarray(scaled.reshape(k // 512, 128, 4, n).transpose(0, 1, 3, 2))
    if fmt == "e4m3":
        words = by_word.astype(ml_dtypes.float8_e4m3fn).view(np.uint8)
    else:
        c = by_word.astype(ml_dtypes.float4_e2m1fn).view(np.uint8) & 0xF
        words = (c[..., 0::2] | (c[..., 1::2] << 4)).reshape(k // 512, 128, 2 * n)
    return np.ascontiguousarray(words), np.ascontiguousarray(byte.astype(np.uint8).reshape(k // 512, 16, n))


def unpack_weight(words, scales, fmt):
    g, _, n = scales.shape
    words = np.ascontiguousarray(words).reshape(g, 128, n, -1)
    if fmt == "e4m3":
        vals = words.view(ml_dtypes.float8_e4m3fn).astype(np.float64)
    else:
        nib = np.empty((g, 128, n, 4), np.uint8)
        nib[..., 0::2] = words & 0xF
        nib[..., 1::2] = words >> 4
        vals = E2M1[nib]
    vals = vals * np.repeat(np.exp2(scales.astype(np.float64) - 127.0), 8, axis=1)[..., None]
    return vals.transpose(0, 1, 3, 2).reshape(g * 512, n)


D, K, R, T, I, Q, G = 512, 512, 512, 2048, 512, 128, 64


def setup_inputs():
    n = np.random.standard_normal
    idx = np.random.permutation(T)[:I]
    fd = mx_kscale(D)
    fk = mx_kscale(K)
    fr = mx_kscale(R)
    keysp = pack_weight(n((D, T)) / fd[:, None], "e2m1")
    tabp = pack_weight(n((K, T)) / fk[:, None], "e2m1")
    return {
        "query": (n((D, Q)) * 0.6 / np.sqrt(D) * fd[:, None]).astype(np.float32),
        "keys_words": keysp[0],
        "keys_scales": keysp[1],
        "sharp": (np.random.uniform(1.0, 3.0, (Q, 1))).astype(np.float32),
        "tab_words": tabp[0],
        "tab_scales": tabp[1],
        "w1": (n((K, R)) * 1 / np.sqrt(K) * fk[:, None]).astype(np.float32),
        "temper": (np.random.uniform(0.4, 1.0, (R, 1))).astype(np.float32),
        "gout": (n((R, Q)) * 1 / np.sqrt(R) * fr[:, None]).astype(np.float32),
        "hsc": (np.random.uniform(0.7, 1.4, (R, 1)) / fr[:, None]).astype(np.float32),
        "old": (0.5 * n((Q, T))).astype(np.float32),
        "offs": striped(idx),
    }


def reference(query, keys_words, keys_scales, sharp, tab_words, tab_scales, w1, temper, gout, hsc, old, offs):
    idx = unstriped(offs)
    keysu = unpack_weight(keys_words, keys_scales, "e2m1")
    tabu = unpack_weight(tab_words, tab_scales, "e2m1")
    queryq = mxq(f64(query), 0, "e4m3")
    keysidxg = keysu[:, idx]
    a = queryq.T @ keysidxg
    p = np.exp(a)
    s = p.reshape(Q, G, I // G).sum(axis=2)
    ms = a.reshape(Q, G, I // G).mean(axis=2) * f64(sharp)
    pg = np.exp(ms - np.max(ms, axis=1, keepdims=True))
    z = np.sum(pg, axis=1, keepdims=True)
    sh = pg / z / s
    rr = np.repeat(sh, I // G, axis=1)
    w1q = mxq(f64(w1), 0, "e4m3")
    tabidxg = tabu[:, idx]
    zh = w1q.T @ tabidxg
    ht = np.exp(zh * f64(temper))
    mz = ht.reshape(R, G, I // G).sum(axis=2)
    mzr = np.repeat(mz, I // G, axis=1)
    hv = ht / mzr * 4.0
    hs1 = hv * f64(hsc)
    goutq = mxq(f64(gout), 0, "e4m3")
    hs1q = mxq(hs1, 0, "e4m3")
    c0 = goutq.T @ hs1q
    drr = c0 * p
    dsh = drr.reshape(Q, G, I // G).sum(axis=2)
    dz = np.sum(dsh / s * pg / np.square(z) * (-1.0), axis=1, keepdims=True)
    dpg = dsh / s / z + dz
    dms = dpg * pg
    e1 = dms * f64(sharp) / 8.0
    r1 = np.repeat(e1, I // G, axis=1)
    ds = dsh * pg / z / np.square(s) * (-1.0)
    r2 = np.repeat(ds, I // G, axis=1)
    dp = c0 * rr + r2
    da = r1 + dp * p
    gs = da * 512.0
    gf = np.zeros((Q, T))
    gf[:, idx] = gs
    y = f64(old) + gf
    return y

@@ -1,0 +1,270 @@
+from contextlib import ExitStack
+
+import concourse.mybir as mybir
+from concourse.masks import make_identity
+
+D, K, R, T, I, Q, G = 512, 512, 512, 2048, 512, 128, 64
+FLOPS = 2 * D * Q * I + 2 * K * R * I + 2 * R * Q * I
+
+F32 = mybir.dt.float32
+BF16 = mybir.dt.bfloat16
+I32 = mybir.dt.int32
+U32 = mybir.dt.uint32
+U16 = mybir.dt.uint16
+U8 = mybir.dt.uint8
+FP8X4 = mybir.dt.float8_e4m3fn_x4
+FP4X4 = mybir.dt.float4_e2m1fn_x4
+ALU = mybir.AluOpType
+ACT = mybir.ActivationFunctionType
+AX = mybir.AxisListType
+
+P = 128
+PACK = 4
+GS = 8
+HALF = I // 2
+GH = G // 2
+
+
+def tile_attend_blrshared_bygroup_kernel(
+    tc, query, keys_words, keys_scales, sharp, tab_words, tab_scales, w1, temper, gout, hsc, old, offs, out
+):
+    nc = tc.nc
+    with ExitStack() as ctx:
+        sb = ctx.enter_context(tc.tile_pool(name="sb", bufs=1))
+        shared = ctx.enter_context(tc.tile_pool(name="shared", bufs=1))
+        ps = ctx.enter_context(tc.psum_pool(name="ps", bufs=1))
+
+        offsets = sb.tile([P, I // 16], U16, name="offsets")
+        nc.sync.dma_start(offsets[:], offs)
+
+        def load_scale_window(src, name):
+            win = sb.tile([P, T], U8, name=name)
+            nc.gpsimd.memset(win[:].bitcast(I32), 0)
+            for quad in range(4):
+                nc.sync.dma_start(
+                    win[32 * quad : 32 * quad + 4, :].bitcast(I32),
+                    src[0, 4 * quad : 4 * quad + 4, :].bitcast(I32),
+                )
+            return win
+
+        def load_word_window(src, name):
+            win = sb.tile([P, T], U16, name=name)
+            nc.sync.dma_start(win[:].bitcast(I32), src[0].bitcast(I32))
+            return win
+
+        def gather(picked, win):
+            nc.vector.tensor_copy(picked[:], win[:].indirect(offsets[:]))
+            return picked
+
+        def quantize(grouped, words, name):
+            codes = sb.tile([P, words], U32, name=name + "_codes", align_bytes=64)
+            scales = sb.tile([P, words], U8, name=name + "_scales", align_bytes=64)
+            nc.vector.quantize_mx(out=codes[:].bitcast(FP8X4), scales=scales[:], in_=grouped)
+            return codes, scales
+
+        tab_scale_win = load_scale_window(tab_scales, "tab_scale_win")
+        tab_word_win = load_word_window(tab_words, "tab_word_win")
+        w1_rows = w1.rearrange("(p j) c -> p j c", j=PACK)
+        w1_raw = []
+        for h in range(2):
+            raw = sb.tile([P, PACK, R // 2], F32, name="w1_raw%d" % h, tag="wide%d" % h)
+            nc.sync.dma_start(raw[:], w1_rows[:, :, h * (R // 2) : (h + 1) * (R // 2)])
+            w1_raw.append(raw)
+        key_scale_win = load_scale_window(keys_scales, "key_scale_win")
+        key_word_win = load_word_window(keys_words, "key_word_win")
+        query_raw = sb.tile([P, PACK, Q], F32, name="query_raw", tag="narrow")
+        nc.sync.dma_start(query_raw[:], query.rearrange("(p j) q -> p j q", j=PACK))
+
+        temper_sb = sb.tile([P, PACK], F32, name="temper_sb")
+        nc.gpsimd.dma_start(temper_sb[:], temper.rearrange("(p t) o -> p (t o)", t=PACK))
+        sharp_sb = sb.tile([P, 1], F32, name="sharp_sb")
+        nc.gpsimd.dma_start(sharp_sb[:], sharp)
+        hsc_sb = sb.tile([P, PACK], F32, name="hsc_sb")
+        nc.gpsimd.dma_start(hsc_sb[:], hsc.rearrange("(p t) o -> p (t o)", t=PACK))
+        ident = sb.tile([P, P], F32, name="ident")
+        make_identity(nc, ident[:])
+
+        gf = sb.tile([P, T], F32, name="gf")
+        nc.vector.memset(gf[:], 0.0)
+
+        w1_grouped = shared.tile([P, PACK, P, PACK], BF16, name="w1_grouped", align_bytes=64, offset=0)
+
+        def deal_views(h):
+            dst = w1_grouped[:, :, 64 * h : 64 * (h + 1), :].rearrange("p t m j -> p m t j")
+            src = w1_raw[h][:].rearrange("p j (m t) -> p m t j", t=PACK)
+            return dst, src
+
+        dst, src = deal_views(0)
+        nc.scalar.activation(dst, src, ACT.Copy)
+        tab_scale = gather(sb.tile([P, I], U8, name="tab_scale", align_bytes=64), tab_scale_win)
+        tab_word = gather(sb.tile([P, I], U16, name="tab_word", align_bytes=64), tab_word_win)
+        dst, src = deal_views(1)
+        nc.vector.tensor_copy(dst, src)
+        w1_q = [
+            quantize(w1_grouped[:, t].rearrange("p m j -> p (m j)"), P, "w1_%d" % t) for t in range(PACK)
+        ]
+        query_grouped = sb.tile([P, Q, PACK], BF16, name="query_grouped", align_bytes=64)
+        nc.scalar.activation(query_grouped[:], query_raw[:].rearrange("p j q -> p q j"), ACT.Copy)
+
+        zh = [ps.tile([P, 2, HALF], F32, name="zh%d" % t, tag="bank%d" % t) for t in range(PACK)]
+        ht = [sb.tile([P, GS, GH // 4, PACK, 4], F32, name="ht%d" % h) for h in range(2)]
+        for h in range(2):
+            cols = slice(h * HALF, (h + 1) * HALF)
+            for t in range(PACK):
+                nc.tensor.matmul_mx(
+                    out=zh[t][:, h, :],
+                    lhsT=w1_q[t][0][:].bitcast(FP8X4),
+                    lhsT_scale=w1_q[t][1][:],
+                    rhs=tab_word[:, cols].bitcast(FP4X4),
+                    rhs_scale=tab_scale[:, cols],
+                    start=True,
+                    stop=True,
+                )
+                nc.scalar.activation(
+                    ht[h][:, :, :, t, :],
+                    zh[t][:, h, :].rearrange("p (c u j) -> p j c u", u=4, j=GS),
+                    ACT.Exp,
+                    scale=temper_sb[:, t : t + 1],
+                )
+
+        key_scale = gather(shared.tile([P, I], U8, name="key_scale", align_bytes=64, offset=0), key_scale_win)
+        key_word = gather(shared.tile([P, I], U16, name="key_word", align_bytes=64, offset=1024), key_word_win)
+        query_q = quantize(query_grouped[:].rearrange("p q j -> p (q j)"), Q, "query")
+
+        def sum_groups_turned(h):
+            acc = ps.tile([P, P], F32, name="mz_turned%d" % h, tag="bank%d" % (5 + h))
+            for j in range(GS):
+                nc.tensor.matmul(
+                    acc[:],
+                    lhsT=ht[h][:, j].rearrange("p c t u -> p (c t u)"),
+                    rhs=ident[:],
+                    is_transpose=True,
+                    start=(j == 0),
+                    stop=(j == GS - 1),
+                )
+            return acc
+
+        mz_turned = [sum_groups_turned(0)]
+        a = ps.tile([P, I], F32, name="a", tag="bank4")
+        nc.tensor.matmul_mx(
+            out=a[:],
+            lhsT=query_q[0][:].bitcast(FP8X4),
+            lhsT_scale=query_q[1][:],
+            rhs=key_word[:].bitcast(FP4X4),
+            rhs_scale=key_scale[:],
+            start=True,
+            stop=True,
+        )
+        mz_turned.append(sum_groups_turned(1))
+        p = sb.tile([P, G, GS], F32, name="p")
+        nc.scalar.activation(p[:].rearrange("p g j -> p (g j)"), a[:], ACT.Exp)
+
+        hsc4 = sb.tile([P, PACK], F32, name="hsc4")
+        nc.gpsimd.tensor_scalar(hsc4[:], hsc_sb[:], 4.0, 0.0, ALU.mult, ALU.add)
+        neg_sigma = sb.tile([P, 1], F32, name="neg_sigma")
+        nc.gpsimd.tensor_scalar(neg_sigma[:], sharp_sb[:], -1.0 / GS, 0.0, ALU.mult, ALU.add)
+
+        gout_raw = sb.tile([P, PACK, Q], F32, name="gout_raw", tag="narrow")
+        nc.sync.dma_start(gout_raw[:], gout.rearrange("(p j) q -> p j q", j=PACK))
+        old_sb = []
+        for h in range(2):
+            tile = sb.tile([P, T // 2], F32, name="old%d" % h, tag="wide%d" % h)
+            nc.sync.dma_start(tile[:], old[:, h * (T // 2) : (h + 1) * (T // 2)])
+            old_sb.append(tile)
+
+        factor = []
+        for h in range(2):
+            inv_turned = sb.tile([P, P], F32, name="inv_turned%d" % h)
+            nc.vector.reciprocal(inv_turned[:], mz_turned[h][:])
+            inv = ps.tile([P, P], F32, name="inv%d" % h, tag="bank%d" % (2 + h))
+            nc.tensor.transpose(inv[:], inv_turned[:], ident[:])
+            factor.append(inv)
+
+        sum_a = sb.tile([P, G], F32, name="sum_a")
+        nc.vector.tensor_reduce(sum_a[:], a[:].rearrange("p (g j) -> p g j", j=GS), AX.X, ALU.add)
+        neg_ms = sb.tile([P, G], F32, name="neg_ms")
+        neg_max = sb.tile([P, 1], F32, name="neg_max")
+        nc.vector.tensor_scalar(neg_ms[:], sum_a[:], neg_sigma[:], None, ALU.mult, ALU.min, accum_out=neg_max[:])
+        pg = sb.tile([P, G], F32, name="pg")
+        z = sb.tile([P, 1], F32, name="z")
+        nc.scalar.activation(pg[:], neg_ms[:], ACT.Exp, bias=neg_max[:], scale=-1.0, accum_out=z[:])
+        s = sb.tile([P, G], F32, name="s")
+        nc.vector.tensor_reduce(s[:], p[:], AX.X, ALU.add)
+
+        gout_grouped = sb.tile([P, Q, PACK], BF16, name="gout_grouped", align_bytes=64)
+        nc.scalar.activation(gout_grouped[:], gout_raw[:].rearrange("p j q -> p q j"), ACT.Copy)
+
+        def by_group(v):
+            return v.unsqueeze(2).to_broadcast([P, v.shape[1], GS])
+
+        hs1_q = []
+        for h in range(2):
+            f = sb.tile([P, GH // 4, PACK, 4], F32, name="f%d" % h)
+            nc.vector.tensor_tensor(
+                f[:],
+                factor[h][:].rearrange("p (c t u) -> p c t u", t=PACK, u=4),
+                hsc4[:].unsqueeze(1).unsqueeze(3).to_broadcast([P, GH // 4, PACK, 4]),
+                ALU.mult,
+            )
+            if h == 0:
+                inv_s = sb.tile([P, G], F32, name="inv_s")
+                nc.vector.reciprocal(inv_s[:], s[:])
+            hs1 = sb.tile([P, GS, GH // 4, 4, PACK], BF16, name="hs1_%d" % h, align_bytes=64)
+            nc.vector.tensor_tensor(
+                hs1[:].rearrange("p j c u t -> p j c t u"),
+                ht[h][:],
+                f[:].unsqueeze(1).to_broadcast([P, GS, GH // 4, PACK, 4]),
+                ALU.mult,
+            )
+            if h == 0:
+                inv_z = sb.tile([P, 1], F32, name="inv_z")
+                nc.vector.reciprocal(inv_z[:], z[:])
+                gout_q = quantize(gout_grouped[:].rearrange("p q j -> p (q j)"), Q, "gout")
+                pi = sb.tile([P, G], F32, name="pi")
+                nc.vector.tensor_scalar(pi[:], pg[:], inv_z[:], None, ALU.mult)
+            hs1_q.append(quantize(hs1[:].rearrange("p j c u t -> p (j c u t)"), HALF, "hs1_%d" % h))
+            if h == 0:
+                alpha = sb.tile([P, G], F32, name="alpha")
+                nc.vector.scalar_tensor_tensor(alpha[:], pi[:], 512.0, inv_s[:], ALU.mult, ALU.mult)
+                u = sb.tile([P, G, GS], F32, name="u")
+                nc.vector.tensor_tensor(u[:], p[:], by_group(alpha[:]), ALU.mult)
+
+        x = sb.tile([P, G, GS], F32, name="x")
+        w = sb.tile([P, G], F32, name="w")
+        beta = sb.tile([P, G], F32, name="beta")
+        p_beta = sb.tile([P, G, GS], F32, name="p_beta")
+        for h in range(2):
+            groups = slice(h * GH, (h + 1) * GH)
+            c0 = ps.tile([P, HALF], F32, name="c0_%d" % h, tag="bank%d" % h)
+            nc.tensor.matmul_mx(
+                out=c0[:],
+                lhsT=gout_q[0][:].bitcast(FP8X4),
+                lhsT_scale=gout_q[1][:],
+                rhs=hs1_q[h][0][:].bitcast(FP8X4),
+                rhs_scale=hs1_q[h][1][:],
+                start=True,
+                stop=True,
+            )
+            nc.vector.tensor_tensor(
+                x[:, groups, :], c0[:].rearrange("p (j g) -> p g j", j=GS), u[:, groups, :], ALU.mult
+            )
+            nc.vector.tensor_reduce(w[:, groups], x[:, groups, :], AX.X, ALU.add)
+            nc.vector.scalar_tensor_tensor(beta[:, groups], w[:, groups], -1.0, inv_s[:, groups], ALU.mult, ALU.mult)
+            nc.vector.tensor_tensor(p_beta[:, groups, :], p[:, groups, :], by_group(beta[:, groups]), ALU.mult)
+        neg_sw = sb.tile([P, G], F32, name="neg_sw")
+        neg_sw_total = sb.tile([P, 1], F32, name="neg_sw_total")
+        nc.vector.tensor_scalar(neg_sw[:], w[:], neg_sigma[:], None, ALU.mult, ALU.add, accum_out=neg_sw_total[:])
+        gamma = sb.tile([P, G], F32, name="gamma")
+        nc.vector.scalar_tensor_tensor(gamma[:], pi[:], neg_sw_total[:], neg_sw[:], ALU.mult, ALU.subtract)
+        x_gamma = sb.tile([P, G, GS], F32, name="x_gamma")
+        nc.vector.tensor_tensor(x_gamma[:], x[:], by_group(gamma[:]), ALU.add)
+        nc.vector.tensor_tensor(
+            gf[:].indirect(offsets[:]),
+            p_beta[:].rearrange("p g j -> p (g j)"),
+            x_gamma[:].rearrange("p g j -> p (g j)"),
+            ALU.add,
+        )
+        for c in range(4):
+            part = old_sb[c // 2][:, (c % 2) * 512 : (c % 2 + 1) * 512]
+            nc.vector.tensor_tensor(part, part, gf[:, c * 512 : (c + 1) * 512], ALU.add)
+            nc.sync.dma_start(out[:, c * 512 : (c + 1) * 512], part)

@@ -23,6 +23,7 @@ PACK = 4
 GS = 8
 HALF = I // 2
 GH = G // 2
+W1_PIECES = ((0, 256), (256, 384), (384, 512))
 
 
 def tile_attend_blrshared_bygroup_kernel(
@@ -37,9 +38,9 @@ def tile_attend_blrshared_bygroup_kernel(
         offsets = sb.tile([P, I // 16], U16, name="offsets")
         nc.sync.dma_start(offsets[:], offs)
 
-        def load_scale_window(src, name):
+        def load_scale_window(src, name, engine):
             win = sb.tile([P, T], U8, name=name)
-            nc.gpsimd.memset(win[:].bitcast(I32), 0)
+            engine.memset(win[:].bitcast(I32), 0)
             for quad in range(4):
                 nc.sync.dma_start(
                     win[32 * quad : 32 * quad + 4, :].bitcast(I32),
@@ -62,49 +63,98 @@ def tile_attend_blrshared_bygroup_kernel(
             nc.vector.quantize_mx(out=codes[:].bitcast(FP8X4), scales=scales[:], in_=grouped)
             return codes, scales
 
-        tab_scale_win = load_scale_window(tab_scales, "tab_scale_win")
-        tab_word_win = load_word_window(tab_words, "tab_word_win")
-        w1_rows = w1.rearrange("(p j) c -> p j c", j=PACK)
-        w1_raw = []
-        for h in range(2):
-            raw = sb.tile([P, PACK, R // 2], F32, name="w1_raw%d" % h, tag="wide%d" % h)
-            nc.sync.dma_start(raw[:], w1_rows[:, :, h * (R // 2) : (h + 1) * (R // 2)])
-            w1_raw.append(raw)
-        key_scale_win = load_scale_window(keys_scales, "key_scale_win")
+        key_scale_win = load_scale_window(keys_scales, "key_scale_win", nc.gpsimd)
         key_word_win = load_word_window(keys_words, "key_word_win")
+        tab_word_win = load_word_window(tab_words, "tab_word_win")
         query_raw = sb.tile([P, PACK, Q], F32, name="query_raw", tag="narrow")
         nc.sync.dma_start(query_raw[:], query.rearrange("(p j) q -> p j q", j=PACK))
+        tab_scale_win = load_scale_window(tab_scales, "tab_scale_win", nc.gpsimd)
+        w1_rows = w1.rearrange("(p j) c -> p j c", j=PACK)
+        w1_raw = []
+        for piece, (first, last) in enumerate(W1_PIECES):
+            if piece == 1:
+                raw = shared.tile([P, PACK, last - first], F32, name="w1_raw1", align_bytes=64, offset=8192)
+            else:
+                raw = sb.tile([P, PACK, last - first], F32, name="w1_raw%d" % piece, tag="wide%d" % piece)
+            nc.sync.dma_start(raw[:], w1_rows[:, :, first:last])
+            w1_raw.append(raw)
 
-        temper_sb = sb.tile([P, PACK], F32, name="temper_sb")
-        nc.gpsimd.dma_start(temper_sb[:], temper.rearrange("(p t) o -> p (t o)", t=PACK))
         sharp_sb = sb.tile([P, 1], F32, name="sharp_sb")
         nc.gpsimd.dma_start(sharp_sb[:], sharp)
+        temper_sb = sb.tile([P, PACK], F32, name="temper_sb")
+        nc.gpsimd.dma_start(temper_sb[:], temper.rearrange("(p t) o -> p (t o)", t=PACK))
         hsc_sb = sb.tile([P, PACK], F32, name="hsc_sb")
         nc.gpsimd.dma_start(hsc_sb[:], hsc.rearrange("(p t) o -> p (t o)", t=PACK))
         ident = sb.tile([P, P], F32, name="ident")
         make_identity(nc, ident[:])
 
+        hsc4 = sb.tile([P, PACK], F32, name="hsc4")
+        nc.gpsimd.tensor_scalar(hsc4[:], hsc_sb[:], 4.0, 0.0, ALU.mult, ALU.add)
+        neg_sigma = sb.tile([P, 1], F32, name="neg_sigma")
+        nc.gpsimd.tensor_scalar(neg_sigma[:], sharp_sb[:], -1.0 / GS, 0.0, ALU.mult, ALU.add)
+        neg_sigma512 = sb.tile([P, 1], F32, name="neg_sigma512")
+        nc.gpsimd.tensor_scalar(neg_sigma512[:], sharp_sb[:], -512.0 / GS, 0.0, ALU.mult, ALU.add)
+
         gf = sb.tile([P, T], F32, name="gf")
         nc.vector.memset(gf[:], 0.0)
 
+        key_scale = gather(sb.tile([P, I], U8, name="key_scale", align_bytes=64), key_scale_win)
+        key_word = gather(sb.tile([P, I], U16, name="key_word", align_bytes=64), key_word_win)
+        tab_word = gather(sb.tile([P, I], U16, name="tab_word", align_bytes=64), tab_word_win)
+        query_grouped = shared.tile([P, Q, PACK], BF16, name="query_grouped", align_bytes=64, offset=4096)
+        nc.scalar.activation(query_grouped[:], query_raw[:].rearrange("p j q -> p q j"), ACT.Copy)
+        query_q = quantize(query_grouped[:].rearrange("p q j -> p (q j)"), Q, "query")
+        tab_scale = gather(shared.tile([P, I], U8, name="tab_scale", align_bytes=64, offset=4096), tab_scale_win)
+        a = ps.tile([P, I], F32, name="a", tag="bank4")
+        nc.tensor.matmul_mx(
+            out=a[:],
+            lhsT=query_q[0][:].bitcast(FP8X4),
+            lhsT_scale=query_q[1][:],
+            rhs=key_word[:].bitcast(FP4X4),
+            rhs_scale=key_scale[:],
+            start=True,
+            stop=True,
+        )
         w1_grouped = shared.tile([P, PACK, P, PACK], BF16, name="w1_grouped", align_bytes=64, offset=0)
 
-        def deal_views(h):
-            dst = w1_grouped[:, :, 64 * h : 64 * (h + 1), :].rearrange("p t m j -> p m t j")
-            src = w1_raw[h][:].rearrange("p j (m t) -> p m t j", t=PACK)
+        def deal_views(piece):
+            first, last = W1_PIECES[piece]
+            dst = w1_grouped[:, :, first // PACK : last // PACK, :].rearrange("p t m j -> p m t j")
+            src = w1_raw[piece][:].rearrange("p j (m t) -> p m t j", t=PACK)
             return dst, src
 
-        dst, src = deal_views(0)
-        nc.scalar.activation(dst, src, ACT.Copy)
-        tab_scale = gather(sb.tile([P, I], U8, name="tab_scale", align_bytes=64), tab_scale_win)
-        tab_word = gather(sb.tile([P, I], U16, name="tab_word", align_bytes=64), tab_word_win)
-        dst, src = deal_views(1)
-        nc.vector.tensor_copy(dst, src)
+        for piece in range(2):
+            nc.scalar.activation(*deal_views(piece), ACT.Copy)
+        nc.vector.tensor_copy(*deal_views(2))
         w1_q = [
-            quantize(w1_grouped[:, t].rearrange("p m j -> p (m j)"), P, "w1_%d" % t) for t in range(PACK)
+            quantize(w1_grouped[:, 2 * pair : 2 * pair + 2].rearrange("p t m j -> p (t m j)"), 2 * P, "w1_%d" % pair)
+            for pair in range(2)
         ]
-        query_grouped = sb.tile([P, Q, PACK], BF16, name="query_grouped", align_bytes=64)
-        nc.scalar.activation(query_grouped[:], query_raw[:].rearrange("p j q -> p q j"), ACT.Copy)
+        p = shared.tile([P, G, GS], F32, name="p", align_bytes=64, offset=8192)
+        nc.scalar.activation(p[:].rearrange("p g j -> p (g j)"), a[:], ACT.Exp)
+
+        def by_group(v):
+            return v.unsqueeze(2).to_broadcast([P, v.shape[1], GS])
+
+        sum_a = shared.tile([P, G], F32, name="sum_a", align_bytes=64, offset=0)
+        nc.vector.tensor_reduce(sum_a[:], a[:].rearrange("p (g j) -> p g j", j=GS), AX.X, ALU.add)
+        neg_ms = sb.tile([P, G], F32, name="neg_ms")
+        neg_max = sb.tile([P, 1], F32, name="neg_max")
+        nc.vector.tensor_scalar(neg_ms[:], sum_a[:], neg_sigma[:], None, ALU.mult, ALU.min, accum_out=neg_max[:])
+        pg = sb.tile([P, G], F32, name="pg")
+        z = sb.tile([P, 1], F32, name="z")
+        nc.scalar.activation(pg[:], neg_ms[:], ACT.Exp, bias=neg_max[:], scale=-1.0, accum_out=z[:])
+
+        s = shared.tile([P, G], F32, name="s", align_bytes=64, offset=256)
+        nc.vector.tensor_reduce(s[:], p[:], AX.X, ALU.add)
+        inv_s = sb.tile([P, G], F32, name="inv_s")
+        nc.vector.reciprocal(inv_s[:], s[:])
+        inv_z = sb.tile([P, 1], F32, name="inv_z")
+        nc.vector.reciprocal(inv_z[:], z[:])
+        alpha = shared.tile([P, G], F32, name="alpha", align_bytes=64, offset=6144 + 384)
+        nc.vector.scalar_tensor_tensor(alpha[:], pg[:], inv_z[:], inv_s[:], ALU.mult, ALU.mult)
+        u = sb.tile([P, G, GS], F32, name="u")
+        nc.vector.tensor_tensor(u[:], p[:], by_group(alpha[:]), ALU.mult)
 
         zh = [ps.tile([P, 2, HALF], F32, name="zh%d" % t, tag="bank%d" % t) for t in range(PACK)]
         ht = [sb.tile([P, GS, GH // 4, PACK, 4], F32, name="ht%d" % h) for h in range(2)]
@@ -113,8 +163,8 @@ def tile_attend_blrshared_bygroup_kernel(
             for t in range(PACK):
                 nc.tensor.matmul_mx(
                     out=zh[t][:, h, :],
-                    lhsT=w1_q[t][0][:].bitcast(FP8X4),
-                    lhsT_scale=w1_q[t][1][:],
+                    lhsT=w1_q[t // 2][0][:, (t % 2) * P : (t % 2 + 1) * P].bitcast(FP8X4),
+                    lhsT_scale=w1_q[t // 2][1][:, (t % 2) * P : (t % 2 + 1) * P],
                     rhs=tab_word[:, cols].bitcast(FP4X4),
                     rhs_scale=tab_scale[:, cols],
                     start=True,
@@ -126,10 +176,6 @@ def tile_attend_blrshared_bygroup_kernel(
                     ACT.Exp,
                     scale=temper_sb[:, t : t + 1],
                 )
-
-        key_scale = gather(shared.tile([P, I], U8, name="key_scale", align_bytes=64, offset=0), key_scale_win)
-        key_word = gather(shared.tile([P, I], U16, name="key_word", align_bytes=64, offset=1024), key_word_win)
-        query_q = quantize(query_grouped[:].rearrange("p q j -> p (q j)"), Q, "query")
 
         def sum_groups_turned(h):
             acc = ps.tile([P, P], F32, name="mz_turned%d" % h, tag="bank%d" % (5 + h))
@@ -144,90 +190,51 @@ def tile_attend_blrshared_bygroup_kernel(
                 )
             return acc
 
+        def scale_features(h):
+            scaled = sb.tile([P, GS, GH // 4, PACK, 4], F32, name="ht_scaled%d" % h)
+            for t in range(PACK):
+                nc.scalar.activation(scaled[:, :, :, t, :], ht[h][:, :, :, t, :], ACT.Copy, scale=hsc4[:, t : t + 1])
+            return scaled
+
+        ht_scaled = [scale_features(0)]
         mz_turned = [sum_groups_turned(0)]
-        a = ps.tile([P, I], F32, name="a", tag="bank4")
-        nc.tensor.matmul_mx(
-            out=a[:],
-            lhsT=query_q[0][:].bitcast(FP8X4),
-            lhsT_scale=query_q[1][:],
-            rhs=key_word[:].bitcast(FP4X4),
-            rhs_scale=key_scale[:],
-            start=True,
-            stop=True,
-        )
         mz_turned.append(sum_groups_turned(1))
-        p = sb.tile([P, G, GS], F32, name="p")
-        nc.scalar.activation(p[:].rearrange("p g j -> p (g j)"), a[:], ACT.Exp)
-
-        hsc4 = sb.tile([P, PACK], F32, name="hsc4")
-        nc.gpsimd.tensor_scalar(hsc4[:], hsc_sb[:], 4.0, 0.0, ALU.mult, ALU.add)
-        neg_sigma = sb.tile([P, 1], F32, name="neg_sigma")
-        nc.gpsimd.tensor_scalar(neg_sigma[:], sharp_sb[:], -1.0 / GS, 0.0, ALU.mult, ALU.add)
-
-        gout_raw = sb.tile([P, PACK, Q], F32, name="gout_raw", tag="narrow")
+        gout_raw = shared.tile([P, PACK, Q], F32, name="gout_raw", align_bytes=64, offset=1024)
         nc.sync.dma_start(gout_raw[:], gout.rearrange("(p j) q -> p j q", j=PACK))
         old_sb = []
-        for h in range(2):
-            tile = sb.tile([P, T // 2], F32, name="old%d" % h, tag="wide%d" % h)
-            nc.sync.dma_start(tile[:], old[:, h * (T // 2) : (h + 1) * (T // 2)])
+        for piece, (first, last) in enumerate(W1_PIECES):
+            tile = sb.tile([P, PACK * (last - first)], F32, name="old%d" % piece, tag=("wide0", "narrow", "wide2")[piece])
+            nc.sync.dma_start(tile[:], old[:, PACK * first : PACK * last])
             old_sb.append(tile)
+        old_parts = [old_sb[0][:, :512], old_sb[0][:, 512:], old_sb[1][:], old_sb[2][:]]
 
         factor = []
         for h in range(2):
-            inv_turned = sb.tile([P, P], F32, name="inv_turned%d" % h)
+            inv_turned = shared.tile([P, P], F32, name="inv_turned%d" % h, align_bytes=64, offset=6144 + 512 * h)
             nc.vector.reciprocal(inv_turned[:], mz_turned[h][:])
             inv = ps.tile([P, P], F32, name="inv%d" % h, tag="bank%d" % (2 + h))
             nc.tensor.transpose(inv[:], inv_turned[:], ident[:])
             factor.append(inv)
 
-        sum_a = sb.tile([P, G], F32, name="sum_a")
-        nc.vector.tensor_reduce(sum_a[:], a[:].rearrange("p (g j) -> p g j", j=GS), AX.X, ALU.add)
-        neg_ms = sb.tile([P, G], F32, name="neg_ms")
-        neg_max = sb.tile([P, 1], F32, name="neg_max")
-        nc.vector.tensor_scalar(neg_ms[:], sum_a[:], neg_sigma[:], None, ALU.mult, ALU.min, accum_out=neg_max[:])
-        pg = sb.tile([P, G], F32, name="pg")
-        z = sb.tile([P, 1], F32, name="z")
-        nc.scalar.activation(pg[:], neg_ms[:], ACT.Exp, bias=neg_max[:], scale=-1.0, accum_out=z[:])
-        s = sb.tile([P, G], F32, name="s")
-        nc.vector.tensor_reduce(s[:], p[:], AX.X, ALU.add)
-
         gout_grouped = sb.tile([P, Q, PACK], BF16, name="gout_grouped", align_bytes=64)
         nc.scalar.activation(gout_grouped[:], gout_raw[:].rearrange("p j q -> p q j"), ACT.Copy)
 
-        def by_group(v):
-            return v.unsqueeze(2).to_broadcast([P, v.shape[1], GS])
+        ht_scaled.append(scale_features(1))
+        gout_q = quantize(gout_grouped[:].rearrange("p q j -> p (q j)"), Q, "gout")
+        pi = sb.tile([P, G], F32, name="pi")
+        nc.scalar.activation(pi[:], pg[:], ACT.Copy, scale=inv_z[:])
 
         hs1_q = []
         for h in range(2):
-            f = sb.tile([P, GH // 4, PACK, 4], F32, name="f%d" % h)
-            nc.vector.tensor_tensor(
-                f[:],
-                factor[h][:].rearrange("p (c t u) -> p c t u", t=PACK, u=4),
-                hsc4[:].unsqueeze(1).unsqueeze(3).to_broadcast([P, GH // 4, PACK, 4]),
-                ALU.mult,
-            )
-            if h == 0:
-                inv_s = sb.tile([P, G], F32, name="inv_s")
-                nc.vector.reciprocal(inv_s[:], s[:])
-            hs1 = sb.tile([P, GS, GH // 4, 4, PACK], BF16, name="hs1_%d" % h, align_bytes=64)
+            f = factor[h][:].rearrange("p (c t u) -> p c t u", t=PACK, u=4)
+            hs1 = sb.tile([P, GS, GH // 4, 4, PACK], BF16, name="hs1_%d" % h, tag="hs1_%d" % h, align_bytes=64)
             nc.vector.tensor_tensor(
                 hs1[:].rearrange("p j c u t -> p j c t u"),
-                ht[h][:],
-                f[:].unsqueeze(1).to_broadcast([P, GS, GH // 4, PACK, 4]),
+                ht_scaled[h][:],
+                f.unsqueeze(1).to_broadcast([P, GS, GH // 4, PACK, 4]),
                 ALU.mult,
             )
-            if h == 0:
-                inv_z = sb.tile([P, 1], F32, name="inv_z")
-                nc.vector.reciprocal(inv_z[:], z[:])
-                gout_q = quantize(gout_grouped[:].rearrange("p q j -> p (q j)"), Q, "gout")
-                pi = sb.tile([P, G], F32, name="pi")
-                nc.vector.tensor_scalar(pi[:], pg[:], inv_z[:], None, ALU.mult)
             hs1_q.append(quantize(hs1[:].rearrange("p j c u t -> p (j c u t)"), HALF, "hs1_%d" % h))
-            if h == 0:
-                alpha = sb.tile([P, G], F32, name="alpha")
-                nc.vector.scalar_tensor_tensor(alpha[:], pi[:], 512.0, inv_s[:], ALU.mult, ALU.mult)
-                u = sb.tile([P, G, GS], F32, name="u")
-                nc.vector.tensor_tensor(u[:], p[:], by_group(alpha[:]), ALU.mult)
 
         x = sb.tile([P, G, GS], F32, name="x")
         w = sb.tile([P, G], F32, name="w")
@@ -249,15 +256,15 @@ def tile_attend_blrshared_bygroup_kernel(
                 x[:, groups, :], c0[:].rearrange("p (j g) -> p g j", j=GS), u[:, groups, :], ALU.mult
             )
             nc.vector.tensor_reduce(w[:, groups], x[:, groups, :], AX.X, ALU.add)
-            nc.vector.scalar_tensor_tensor(beta[:, groups], w[:, groups], -1.0, inv_s[:, groups], ALU.mult, ALU.mult)
+            nc.vector.scalar_tensor_tensor(beta[:, groups], w[:, groups], -512.0, inv_s[:, groups], ALU.mult, ALU.mult)
             nc.vector.tensor_tensor(p_beta[:, groups, :], p[:, groups, :], by_group(beta[:, groups]), ALU.mult)
         neg_sw = sb.tile([P, G], F32, name="neg_sw")
         neg_sw_total = sb.tile([P, 1], F32, name="neg_sw_total")
-        nc.vector.tensor_scalar(neg_sw[:], w[:], neg_sigma[:], None, ALU.mult, ALU.add, accum_out=neg_sw_total[:])
+        nc.vector.tensor_scalar(neg_sw[:], w[:], neg_sigma512[:], None, ALU.mult, ALU.add, accum_out=neg_sw_total[:])
         gamma = sb.tile([P, G], F32, name="gamma")
         nc.vector.scalar_tensor_tensor(gamma[:], pi[:], neg_sw_total[:], neg_sw[:], ALU.mult, ALU.subtract)
         x_gamma = sb.tile([P, G, GS], F32, name="x_gamma")
-        nc.vector.tensor_tensor(x_gamma[:], x[:], by_group(gamma[:]), ALU.add)
+        nc.vector.scalar_tensor_tensor(x_gamma[:], x[:], 512.0, by_group(gamma[:]), ALU.mult, ALU.add)
         nc.vector.tensor_tensor(
             gf[:].indirect(offsets[:]),
             p_beta[:].rearrange("p g j -> p (g j)"),
@@ -265,6 +272,6 @@ def tile_attend_blrshared_bygroup_kernel(
             ALU.add,
         )
         for c in range(4):
-            part = old_sb[c // 2][:, (c % 2) * 512 : (c % 2 + 1) * 512]
+            part = old_parts[c]
             nc.vector.tensor_tensor(part, part, gf[:, c * 512 : (c + 1) * 512], ALU.add)
             nc.sync.dma_start(out[:, c * 512 : (c + 1) * 512], part)

from contextlib import ExitStack

import concourse.mybir as mybir
from concourse.masks import make_identity

D, K, R, T, I, Q, G = 512, 512, 512, 2048, 512, 128, 64
FLOPS = 2 * D * Q * I + 2 * K * R * I + 2 * R * Q * I

F32 = mybir.dt.float32
BF16 = mybir.dt.bfloat16
I32 = mybir.dt.int32
U32 = mybir.dt.uint32
U16 = mybir.dt.uint16
U8 = mybir.dt.uint8
FP8X4 = mybir.dt.float8_e4m3fn_x4
FP4X4 = mybir.dt.float4_e2m1fn_x4
ALU = mybir.AluOpType
ACT = mybir.ActivationFunctionType
AX = mybir.AxisListType

P = 128
PACK = 4
GS = 8
HALF = I // 2
GH = G // 2
W1_PIECES = ((0, 256), (256, 384), (384, 512))


def tile_attend_blrshared_bygroup_kernel(
    tc, query, keys_words, keys_scales, sharp, tab_words, tab_scales, w1, temper, gout, hsc, old, offs, out
):
    nc = tc.nc
    with ExitStack() as ctx:
        sb = ctx.enter_context(tc.tile_pool(name="sb", bufs=1))
        shared = ctx.enter_context(tc.tile_pool(name="shared", bufs=1))
        ps = ctx.enter_context(tc.psum_pool(name="ps", bufs=1))

        offsets = sb.tile([P, I // 16], U16, name="offsets")
        nc.sync.dma_start(offsets[:], offs)

        def load_scale_window(src, name, engine):
            win = sb.tile([P, T], U8, name=name)
            engine.memset(win[:].bitcast(I32), 0)
            for quad in range(4):
                nc.sync.dma_start(
                    win[32 * quad : 32 * quad + 4, :].bitcast(I32),
                    src[0, 4 * quad : 4 * quad + 4, :].bitcast(I32),
                )
            return win

        def load_word_window(src, name):
            win = sb.tile([P, T], U16, name=name)
            nc.sync.dma_start(win[:].bitcast(I32), src[0].bitcast(I32))
            return win

        def gather(picked, win):
            nc.vector.tensor_copy(picked[:], win[:].indirect(offsets[:]))
            return picked

        def quantize(grouped, words, name):
            codes = sb.tile([P, words], U32, name=name + "_codes", align_bytes=64)
            scales = sb.tile([P, words], U8, name=name + "_scales", align_bytes=64)
            nc.vector.quantize_mx(out=codes[:].bitcast(FP8X4), scales=scales[:], in_=grouped)
            return codes, scales

        key_scale_win = load_scale_window(keys_scales, "key_scale_win", nc.gpsimd)
        key_word_win = load_word_window(keys_words, "key_word_win")
        tab_word_win = load_word_window(tab_words, "tab_word_win")
        query_raw = sb.tile([P, PACK, Q], F32, name="query_raw", tag="narrow")
        nc.sync.dma_start(query_raw[:], query.rearrange("(p j) q -> p j q", j=PACK))
        tab_scale_win = load_scale_window(tab_scales, "tab_scale_win", nc.gpsimd)
        w1_rows = w1.rearrange("(p j) c -> p j c", j=PACK)
        w1_raw = []
        for piece, (first, last) in enumerate(W1_PIECES):
            if piece == 1:
                raw = shared.tile([P, PACK, last - first], F32, name="w1_raw1", align_bytes=64, offset=8192)
            else:
                raw = sb.tile([P, PACK, last - first], F32, name="w1_raw%d" % piece, tag="wide%d" % piece)
            nc.sync.dma_start(raw[:], w1_rows[:, :, first:last])
            w1_raw.append(raw)

        sharp_sb = sb.tile([P, 1], F32, name="sharp_sb")
        nc.gpsimd.dma_start(sharp_sb[:], sharp)
        temper_sb = sb.tile([P, PACK], F32, name="temper_sb")
        nc.gpsimd.dma_start(temper_sb[:], temper.rearrange("(p t) o -> p (t o)", t=PACK))
        hsc_sb = sb.tile([P, PACK], F32, name="hsc_sb")
        nc.gpsimd.dma_start(hsc_sb[:], hsc.rearrange("(p t) o -> p (t o)", t=PACK))
        ident = sb.tile([P, P], F32, name="ident")
        make_identity(nc, ident[:])

        hsc4 = sb.tile([P, PACK], F32, name="hsc4")
        nc.gpsimd.tensor_scalar(hsc4[:], hsc_sb[:], 4.0, 0.0, ALU.mult, ALU.add)
        neg_sigma = sb.tile([P, 1], F32, name="neg_sigma")
        nc.gpsimd.tensor_scalar(neg_sigma[:], sharp_sb[:], -1.0 / GS, 0.0, ALU.mult, ALU.add)
        neg_sigma512 = sb.tile([P, 1], F32, name="neg_sigma512")
        nc.gpsimd.tensor_scalar(neg_sigma512[:], sharp_sb[:], -512.0 / GS, 0.0, ALU.mult, ALU.add)

        gf = sb.tile([P, T], F32, name="gf")
        nc.vector.memset(gf[:], 0.0)

        key_scale = gather(sb.tile([P, I], U8, name="key_scale", align_bytes=64), key_scale_win)
        key_word = gather(sb.tile([P, I], U16, name="key_word", align_bytes=64), key_word_win)
        tab_word = gather(sb.tile([P, I], U16, name="tab_word", align_bytes=64), tab_word_win)
        query_grouped = shared.tile([P, Q, PACK], BF16, name="query_grouped", align_bytes=64, offset=4096)
        nc.scalar.activation(query_grouped[:], query_raw[:].rearrange("p j q -> p q j"), ACT.Copy)
        query_q = quantize(query_grouped[:].rearrange("p q j -> p (q j)"), Q, "query")
        tab_scale = gather(shared.tile([P, I], U8, name="tab_scale", align_bytes=64, offset=4096), tab_scale_win)
        a = ps.tile([P, I], F32, name="a", tag="bank4")
        nc.tensor.matmul_mx(
            out=a[:],
            lhsT=query_q[0][:].bitcast(FP8X4),
            lhsT_scale=query_q[1][:],
            rhs=key_word[:].bitcast(FP4X4),
            rhs_scale=key_scale[:],
            start=True,
            stop=True,
        )
        w1_grouped = shared.tile([P, PACK, P, PACK], BF16, name="w1_grouped", align_bytes=64, offset=0)

        def deal_views(piece):
            first, last = W1_PIECES[piece]
            dst = w1_grouped[:, :, first // PACK : last // PACK, :].rearrange("p t m j -> p m t j")
            src = w1_raw[piece][:].rearrange("p j (m t) -> p m t j", t=PACK)
            return dst, src

        for piece in range(2):
            nc.scalar.activation(*deal_views(piece), ACT.Copy)
        nc.vector.tensor_copy(*deal_views(2))
        w1_q = [
            quantize(w1_grouped[:, 2 * pair : 2 * pair + 2].rearrange("p t m j -> p (t m j)"), 2 * P, "w1_%d" % pair)
            for pair in range(2)
        ]
        p = shared.tile([P, G, GS], F32, name="p", align_bytes=64, offset=8192)
        nc.scalar.activation(p[:].rearrange("p g j -> p (g j)"), a[:], ACT.Exp)

        def by_group(v):
            return v.unsqueeze(2).to_broadcast([P, v.shape[1], GS])

        sum_a = shared.tile([P, G], F32, name="sum_a", align_bytes=64, offset=0)
        nc.vector.tensor_reduce(sum_a[:], a[:].rearrange("p (g j) -> p g j", j=GS), AX.X, ALU.add)
        neg_ms = sb.tile([P, G], F32, name="neg_ms")
        neg_max = sb.tile([P, 1], F32, name="neg_max")
        nc.vector.tensor_scalar(neg_ms[:], sum_a[:], neg_sigma[:], None, ALU.mult, ALU.min, accum_out=neg_max[:])
        pg = sb.tile([P, G], F32, name="pg")
        z = sb.tile([P, 1], F32, name="z")
        nc.scalar.activation(pg[:], neg_ms[:], ACT.Exp, bias=neg_max[:], scale=-1.0, accum_out=z[:])

        s = shared.tile([P, G], F32, name="s", align_bytes=64, offset=256)
        nc.vector.tensor_reduce(s[:], p[:], AX.X, ALU.add)
        inv_s = sb.tile([P, G], F32, name="inv_s")
        nc.vector.reciprocal(inv_s[:], s[:])
        inv_z = sb.tile([P, 1], F32, name="inv_z")
        nc.vector.reciprocal(inv_z[:], z[:])
        alpha = shared.tile([P, G], F32, name="alpha", align_bytes=64, offset=6144 + 384)
        nc.vector.scalar_tensor_tensor(alpha[:], pg[:], inv_z[:], inv_s[:], ALU.mult, ALU.mult)
        u = sb.tile([P, G, GS], F32, name="u")
        nc.vector.tensor_tensor(u[:], p[:], by_group(alpha[:]), ALU.mult)

        zh = [ps.tile([P, 2, HALF], F32, name="zh%d" % t, tag="bank%d" % t) for t in range(PACK)]
        ht = [sb.tile([P, GS, GH // 4, PACK, 4], F32, name="ht%d" % h) for h in range(2)]
        for h in range(2):
            cols = slice(h * HALF, (h + 1) * HALF)
            for t in range(PACK):
                nc.tensor.matmul_mx(
                    out=zh[t][:, h, :],
                    lhsT=w1_q[t // 2][0][:, (t % 2) * P : (t % 2 + 1) * P].bitcast(FP8X4),
                    lhsT_scale=w1_q[t // 2][1][:, (t % 2) * P : (t % 2 + 1) * P],
                    rhs=tab_word[:, cols].bitcast(FP4X4),
                    rhs_scale=tab_scale[:, cols],
                    start=True,
                    stop=True,
                )
                nc.scalar.activation(
                    ht[h][:, :, :, t, :],
                    zh[t][:, h, :].rearrange("p (c u j) -> p j c u", u=4, j=GS),
                    ACT.Exp,
                    scale=temper_sb[:, t : t + 1],
                )

        def sum_groups_turned(h):
            acc = ps.tile([P, P], F32, name="mz_turned%d" % h, tag="bank%d" % (5 + h))
            for j in range(GS):
                nc.tensor.matmul(
                    acc[:],
                    lhsT=ht[h][:, j].rearrange("p c t u -> p (c t u)"),
                    rhs=ident[:],
                    is_transpose=True,
                    start=(j == 0),
                    stop=(j == GS - 1),
                )
            return acc

        def scale_features(h):
            scaled = sb.tile([P, GS, GH // 4, PACK, 4], F32, name="ht_scaled%d" % h)
            for t in range(PACK):
                nc.scalar.activation(scaled[:, :, :, t, :], ht[h][:, :, :, t, :], ACT.Copy, scale=hsc4[:, t : t + 1])
            return scaled

        ht_scaled = [scale_features(0)]
        mz_turned = [sum_groups_turned(0)]
        mz_turned.append(sum_groups_turned(1))
        gout_raw = shared.tile([P, PACK, Q], F32, name="gout_raw", align_bytes=64, offset=1024)
        nc.sync.dma_start(gout_raw[:], gout.rearrange("(p j) q -> p j q", j=PACK))
        old_sb = []
        for piece, (first, last) in enumerate(W1_PIECES):
            tile = sb.tile([P, PACK * (last - first)], F32, name="old%d" % piece, tag=("wide0", "narrow", "wide2")[piece])
            nc.sync.dma_start(tile[:], old[:, PACK * first : PACK * last])
            old_sb.append(tile)
        old_parts = [old_sb[0][:, :512], old_sb[0][:, 512:], old_sb[1][:], old_sb[2][:]]

        factor = []
        for h in range(2):
            inv_turned = shared.tile([P, P], F32, name="inv_turned%d" % h, align_bytes=64, offset=6144 + 512 * h)
            nc.vector.reciprocal(inv_turned[:], mz_turned[h][:])
            inv = ps.tile([P, P], F32, name="inv%d" % h, tag="bank%d" % (2 + h))
            nc.tensor.transpose(inv[:], inv_turned[:], ident[:])
            factor.append(inv)

        gout_grouped = sb.tile([P, Q, PACK], BF16, name="gout_grouped", align_bytes=64)
        nc.scalar.activation(gout_grouped[:], gout_raw[:].rearrange("p j q -> p q j"), ACT.Copy)

        ht_scaled.append(scale_features(1))
        gout_q = quantize(gout_grouped[:].rearrange("p q j -> p (q j)"), Q, "gout")
        pi = sb.tile([P, G], F32, name="pi")
        nc.scalar.activation(pi[:], pg[:], ACT.Copy, scale=inv_z[:])

        hs1_q = []
        for h in range(2):
            f = factor[h][:].rearrange("p (c t u) -> p c t u", t=PACK, u=4)
            hs1 = sb.tile([P, GS, GH // 4, 4, PACK], BF16, name="hs1_%d" % h, tag="hs1_%d" % h, align_bytes=64)
            nc.vector.tensor_tensor(
                hs1[:].rearrange("p j c u t -> p j c t u"),
                ht_scaled[h][:],
                f.unsqueeze(1).to_broadcast([P, GS, GH // 4, PACK, 4]),
                ALU.mult,
            )
            hs1_q.append(quantize(hs1[:].rearrange("p j c u t -> p (j c u t)"), HALF, "hs1_%d" % h))

        x = sb.tile([P, G, GS], F32, name="x")
        w = sb.tile([P, G], F32, name="w")
        beta = sb.tile([P, G], F32, name="beta")
        p_beta = sb.tile([P, G, GS], F32, name="p_beta")
        for h in range(2):
            groups = slice(h * GH, (h + 1) * GH)
            c0 = ps.tile([P, HALF], F32, name="c0_%d" % h, tag="bank%d" % h)
            nc.tensor.matmul_mx(
                out=c0[:],
                lhsT=gout_q[0][:].bitcast(FP8X4),
                lhsT_scale=gout_q[1][:],
                rhs=hs1_q[h][0][:].bitcast(FP8X4),
                rhs_scale=hs1_q[h][1][:],
                start=True,
                stop=True,
            )
            nc.vector.tensor_tensor(
                x[:, groups, :], c0[:].rearrange("p (j g) -> p g j", j=GS), u[:, groups, :], ALU.mult
            )
            nc.vector.tensor_reduce(w[:, groups], x[:, groups, :], AX.X, ALU.add)
            nc.vector.scalar_tensor_tensor(beta[:, groups], w[:, groups], -512.0, inv_s[:, groups], ALU.mult, ALU.mult)
            nc.vector.tensor_tensor(p_beta[:, groups, :], p[:, groups, :], by_group(beta[:, groups]), ALU.mult)
        neg_sw = sb.tile([P, G], F32, name="neg_sw")
        neg_sw_total = sb.tile([P, 1], F32, name="neg_sw_total")
        nc.vector.tensor_scalar(neg_sw[:], w[:], neg_sigma512[:], None, ALU.mult, ALU.add, accum_out=neg_sw_total[:])
        gamma = sb.tile([P, G], F32, name="gamma")
        nc.vector.scalar_tensor_tensor(gamma[:], pi[:], neg_sw_total[:], neg_sw[:], ALU.mult, ALU.subtract)
        x_gamma = sb.tile([P, G, GS], F32, name="x_gamma")
        nc.vector.scalar_tensor_tensor(x_gamma[:], x[:], 512.0, by_group(gamma[:]), ALU.mult, ALU.add)
        nc.vector.tensor_tensor(
            gf[:].indirect(offsets[:]),
            p_beta[:].rearrange("p g j -> p (g j)"),
            x_gamma[:].rearrange("p g j -> p (g j)"),
            ALU.add,
        )
        for c in range(4):
            part = old_parts[c]
            nc.vector.tensor_tensor(part, part, gf[:, c * 512 : (c + 1) * 512], ALU.add)
            nc.sync.dma_start(out[:, c * 512 : (c + 1) * 512], part)
